import numpy as np, ml_dtypes
CORES = [23,39,55,63,87,103,111,127,18,34,50,58,82,98,106,122]
N = 16
import mx_ref
NC, GR, GC, KT = 256, 4, 4, 1
TS = GC * KT
CH = GR * NC // GC
BF = ml_dtypes.bfloat16
def setup_inputs(rng):
    def f(*shape):
        return mx_ref.flush((rng.standard_normal(shape, dtype=np.float32) * np.exp2(rng.integers(-2, 3, shape[:-1] + (1,)))).astype(BF))
    return {"w": f(N, 128, KT * 512), "x": f(N, 128, KT * 4 * NC)}
def setup_inputs_blocks(rng):
    d = setup_inputs(rng)
    for k in ("w", "x"): d[k] = mx_ref.spread(d[k], rng, 1)
    return d
def setup_inputs_wide(rng):
    d = setup_inputs(rng)
    for k in ("w", "x"): d[k] = mx_ref.flush((d[k].astype(np.float32) * np.exp2(rng.integers(-8, 9, (N, 1, 1))).astype(np.float32)).astype(BF))
    return d
def setup_inputs_zeros(rng):
    d = setup_inputs(rng); v = d["x"].reshape(N, 128, -1, 4).copy()
    v[np.broadcast_to((rng.random((N, 1, v.shape[2], 1)) < 0.33), v.shape)] = 0
    d["x"] = v.reshape(d["x"].shape)
    return d
def reference(w, x):
    QX = [[mx_ref.quantize(x[r][:, 4 * NC * t:4 * NC * t + 4 * NC]) for t in range(KT)] for r in range(N)]
    y = np.zeros((N, 128, CH), np.float32)
    for i in range(GR):
        for s in range(TS):
            k, t = s // KT, s % KT
            qw = mx_ref.quantize(w[i * GC + k][:, 512 * t:512 * t + 512])
            p = np.concatenate([mx_ref.matmul(qw, QX[g * GC + k][t]) for g in range(GR)], axis=1)
            Y = p if s == 0 else Y + p
        for c in range(GC):
            y[i * GC + c] = Y[:, CH * c:CH * c + CH]
    return {"y": y}

@@ -1,0 +1,137 @@
+from concourse.bass import DstId, RemoteDMATransfer
+from concourse.mybir import dt, AluOpType, ActivationFunctionType
+
+GR, GC, NC, BANK = 4, 4, 256, 512
+
+SCRATCH = {
+    "xb": ("sbuf", [128, 4 * NC], "bfloat16"),
+    "wb": ("sbuf", [128, 512], "bfloat16"),
+    "xq": ("sbuf", [128, GR * NC], "float8_e4m3fn_x4"),
+    "xs": ("sbuf", [128, GR * NC], "uint8"),
+    "wq": ("sbuf", [128, 128], "float8_e4m3fn_x4"),
+    "ws": ("sbuf", [128, 128], "uint8"),
+    "ps": ("psum", [128, GR * BANK], "float32"),
+    "pout": ("sbuf", [128, GR * NC], "float32"),
+    "pin": ("sbuf", [128, GC * NC], "float32"),
+    "acc": ("sbuf", [128, NC], "float32"),
+}
+SEMAPHORES = (["lx", "lw", "qx", "qw", "sent", "stored", "a0", "a1", "a2"]
+              + ["c%d" % r for r in range(GR)] + ["s%d" % r for r in range(GR)]
+              + ["mm%d" % r for r in range(GR)] + ["cp%d" % r for r in range(GR)]
+              + ["p%d" % c for c in range(GC)])
+
+
+def _bits(m):
+    return bin(m).count("1")
+
+
+def rank_program(g, core, T, topo):
+    rank = T.rank_of(core)
+    if rank is None:
+        return
+    i, k = divmod(rank, GC)
+    col = [T.cores[r * GC + k] for r in range(GR)]
+    row = [T.cores[i * GC + c] for c in range(GC)]
+    sem = T.sem
+
+    def gate(src, chip):
+        there = [r for r in range(GR) if topo.chip(col[r]) == chip]
+        same_die = [r for r in there if topo.die(col[r]) == topo.die(col[src])]
+        return (same_die or there)[0]
+
+    here = topo.chip(core)
+    near = [r for r in range(GR) if r != i and topo.chip(col[r]) == here]
+    far = [r for r in range(GR) if topo.chip(col[r]) != here]
+    straight = [r for r in far if gate(r, here) == i]
+    passed = [r for r in far if gate(r, here) != i]
+    gates = sorted(set(gate(i, topo.chip(col[r])) for r in far))
+    order = [i] + near + straight + passed
+
+    m_off = topo.mask(core, col[far[0]])
+    for c in range(GC):
+        if c != k:
+            m_off &= topo.mask(core, row[c])
+    m_on = topo.mask(core, col[near[0]]) & ~m_off
+    n_off, n_on = _bits(m_off), _bits(m_on)
+    sent = [0]
+
+    def dst_id(c):
+        rid, pid, _ = topo.addr(c)
+        return DstId(rid=rid, pnc=pid)
+
+    def codes(r):
+        return T.xq[:, r * NC:(r + 1) * NC].bitcast(dt.uint8)
+
+    def plane(r):
+        return T.xs[:, r * NC:(r + 1) * NC]
+
+    def spread(view, name, r, off, on):
+        tr = []
+        for group, m in ((off, m_off), (on, m_on)):
+            if group:
+                tr.append(RemoteDMATransfer(dst_ids=[dst_id(col[d]) for d in group], dma_engine_mask=m,
+                                            remote_sem=sem[name % r], srcs=[view(r)], dsts=[view(r) for d in group]))
+                sent[0] += _bits(m)
+        g.remote_dma_fused(tr, local_sem=sem.sent)
+
+    g.sync.dma_start(T.xb[:], T.x[:]).then_inc(sem.lx, 16)
+    g.scalar.dma_start(T.wb[:], T.w[:]).then_inc(sem.lw, 16)
+    g.vector.wait_ge(sem.lx, 16)
+    g.vector.quantize_mx(T.xq[:, i * NC:(i + 1) * NC], plane(i), T.xb[:]).then_inc(sem.qx, 1)
+    g.vector.wait_ge(sem.lw, 16)
+    g.vector.quantize_mx(T.wq[:], T.ws[:], T.wb[:]).then_inc(sem.qw, 1)
+
+    g.tensor.wait_ge(sem.qx, 1)
+    g.tensor.wait_ge(sem.qw, 1)
+    for r in order:
+        if r != i:
+            n = n_off if r in straight else n_on
+            g.tensor.wait_ge(sem["c%d" % r], n)
+            g.tensor.wait_ge(sem["s%d" % r], n)
+        g.tensor.matmul_mx(T.ps[:, r * BANK:r * BANK + NC], T.wq[:], T.ws[:], T.xq[:, r * NC:(r + 1) * NC], plane(r),
+                           True, True).then_inc(sem["mm%d" % r], 1)
+
+    for r in order:
+        if r != k:
+            g.scalar.wait_ge(sem["mm%d" % r], 1)
+            g.scalar.activation(T.pout[:, r * NC:(r + 1) * NC], T.ps[:, r * BANK:r * BANK + NC],
+                                ActivationFunctionType.Copy).then_inc(sem["cp%d" % r], 1)
+
+    def send_partial(r):
+        if r == k:
+            return
+        rid, pid, _ = topo.addr(row[r])
+        g.wait_ge(sem["cp%d" % r], 1)
+        g.remote_dma(T.pin[:, k * NC:(k + 1) * NC], T.pout[:, r * NC:(r + 1) * NC], sem["p%d" % k], sem.sent,
+                     pid, rid, m_off)
+        sent[0] += n_off
+
+    g.wait_ge(sem.qx, 1)
+    spread(codes, "c%d", i, gates, near)
+    spread(plane, "s%d", i, gates, near)
+    send_partial(i)
+    for r in straight:
+        g.wait_ge(sem["c%d" % r], n_off)
+        spread(codes, "c%d", r, [], near)
+        g.wait_ge(sem["s%d" % r], n_off)
+        spread(plane, "s%d", r, [], near)
+    for r in near + straight + passed:
+        send_partial(r)
+    g.wait_ge(sem.sent, sent[0])
+
+    def hops(c):
+        a, b = topo.chip(row[c]), here
+        return 1 if (topo.mates(a, b) or topo.same_plane(a, b)) else 2
+
+    srcs = sorted([c for c in range(GC) if c != k], key=lambda c: (hops(c), c))
+    g.vector.wait_ge(sem["mm%d" % k], 1)
+    for j, c in enumerate(srcs):
+        g.vector.wait_ge(sem["p%d" % c], n_off)
+        if j:
+            g.vector.wait_ge(sem["a%d" % (j - 1)], 1)
+        first = T.ps[:, k * BANK:k * BANK + NC] if j == 0 else T.acc[:]
+        g.vector.tensor_tensor(T.acc[:], first, T.pin[:, c * NC:(c + 1) * NC], AluOpType.add).then_inc(sem["a%d" % j], 1)
+
+    g.sync.wait_ge(sem["a%d" % (len(srcs) - 1)], 1)
+    g.sync.dma_start(T.y[:], T.acc[:]).then_inc(sem.stored, 16)
+    g.sync.wait_ge(sem.stored, 16)

@@ -10,12 +10,14 @@ SCRATCH = {
     "xs": ("sbuf", [128, GR * NC], "uint8"),
     "wq": ("sbuf", [128, 128], "float8_e4m3fn_x4"),
     "ws": ("sbuf", [128, 128], "uint8"),
+    "wq2": ("sbuf", [128, 128], "float8_e4m3fn_x4"),
+    "ws2": ("sbuf", [128, 128], "uint8"),
     "ps": ("psum", [128, GR * BANK], "float32"),
     "pout": ("sbuf", [128, GR * NC], "float32"),
     "pin": ("sbuf", [128, GC * NC], "float32"),
     "acc": ("sbuf", [128, NC], "float32"),
 }
-SEMAPHORES = (["lx", "lw", "qx", "qw", "sent", "stored", "a0", "a1", "a2"]
+SEMAPHORES = (["lx", "lw", "qx", "qw", "sent", "stored", "a0", "a1", "a2", "wc", "wp"]
               + ["c%d" % r for r in range(GR)] + ["s%d" % r for r in range(GR)]
               + ["mm%d" % r for r in range(GR)] + ["cp%d" % r for r in range(GR)]
               + ["p%d" % c for c in range(GC)])
@@ -30,28 +32,51 @@ def rank_program(g, core, T, topo):
     if rank is None:
         return
     i, k = divmod(rank, GC)
-    col = [T.cores[r * GC + k] for r in range(GR)]
-    row = [T.cores[i * GC + c] for c in range(GC)]
     sem = T.sem
 
-    def gate(src, chip):
-        there = [r for r in range(GR) if topo.chip(col[r]) == chip]
-        same_die = [r for r in there if topo.die(col[r]) == topo.die(col[src])]
-        return (same_die or there)[0]
+    def rk(r, c):
+        return T.cores[r * GC + c]
 
+    def at_home(r, c):
+        return topo.chip(rk(c, c)) == topo.chip(rk(r, c))
+
+    def gate_of(src, takers):
+        same_die = [c for c in takers if topo.die(c) == topo.die(src)]
+        return (same_die or takers)[0]
+
+    col = [rk(r, k) for r in range(GR)]
+    row = [rk(i, c) for c in range(GC)]
     here = topo.chip(core)
+    mine = [c for c in col if topo.chip(c) == here]
     near = [r for r in range(GR) if r != i and topo.chip(col[r]) == here]
     far = [r for r in range(GR) if topo.chip(col[r]) != here]
-    straight = [r for r in far if gate(r, here) == i]
-    passed = [r for r in far if gate(r, here) != i]
-    gates = sorted(set(gate(i, topo.chip(col[r])) for r in far))
-    order = [i] + near + straight + passed
+    home = at_home(i, k)
+    buddies = [col[r] for r in near]
 
-    m_off = topo.mask(core, col[far[0]])
-    for c in range(GC):
-        if c != k:
-            m_off &= topo.mask(core, row[c])
-    m_on = topo.mask(core, col[near[0]]) & ~m_off
+    if home:
+        cross = list(far)
+        src_of = dict((t, rk(t, k)) for t in cross)
+    else:
+        cross = [k] + [s for s in range(GC) if s != k and at_home(k, s)]
+        src_of = dict((t, rk(k, t)) for t in cross)
+    assert sorted(cross) == sorted(far) and len(cross) == 2
+    straight = [t for t in cross if gate_of(src_of[t], mine) == core]
+    passed = [t for t in cross if gate_of(src_of[t], mine) != core]
+
+    if home:
+        takers = [rk(f, i) for f in range(GR) if topo.chip(rk(f, i)) != topo.chip(rk(i, i))]
+        there_slot = k
+    else:
+        takers = [col[f] for f in far]
+        there_slot = i
+    gates = [gate_of(core, [c for c in takers if topo.chip(c) == ch]) for ch in sorted(set(topo.chip(c) for c in takers))]
+    swap = [] if home else [c for c in range(GC) if c != k and not at_home(i, c)]
+
+    m_off = topo.mask(core, buddies[0])
+    for c in T.cores:
+        if topo.chip(c) != here:
+            m_off &= topo.mask(core, c)
+    m_on = topo.mask(core, buddies[0]) & ~m_off
     n_off, n_on = _bits(m_off), _bits(m_on)
     sent = [0]
 
@@ -65,12 +90,13 @@ def rank_program(g, core, T, topo):
     def plane(r):
         return T.xs[:, r * NC:(r + 1) * NC]
 
-    def spread(view, name, r, off, on):
+    def spread(view, name, slot, groups):
         tr = []
-        for group, m in ((off, m_off), (on, m_on)):
-            if group:
-                tr.append(RemoteDMATransfer(dst_ids=[dst_id(col[d]) for d in group], dma_engine_mask=m,
-                                            remote_sem=sem[name % r], srcs=[view(r)], dsts=[view(r) for d in group]))
+        for cores_, m, there in groups:
+            if cores_:
+                tr.append(RemoteDMATransfer(dst_ids=[dst_id(c) for c in cores_], dma_engine_mask=m,
+                                            remote_sem=sem[name % there], srcs=[view(slot)],
+                                            dsts=[view(there) for c in cores_]))
                 sent[0] += _bits(m)
         g.remote_dma_fused(tr, local_sem=sem.sent)
 
@@ -81,17 +107,31 @@ def rank_program(g, core, T, topo):
     g.vector.wait_ge(sem.lw, 16)
     g.vector.quantize_mx(T.wq[:], T.ws[:], T.wb[:]).then_inc(sem.qw, 1)
 
+    def tile_here(t):
+        n = n_off if t in straight else n_on
+        g.tensor.wait_ge(sem["c%d" % t], n)
+        g.tensor.wait_ge(sem["s%d" % t], n)
+
     g.tensor.wait_ge(sem.qx, 1)
     g.tensor.wait_ge(sem.qw, 1)
-    for r in order:
+    shares = [i] + near + (straight + passed if home else [])
+    for r in shares:
         if r != i:
-            n = n_off if r in straight else n_on
-            g.tensor.wait_ge(sem["c%d" % r], n)
-            g.tensor.wait_ge(sem["s%d" % r], n)
+            tile_here(r)
         g.tensor.matmul_mx(T.ps[:, r * BANK:r * BANK + NC], T.wq[:], T.ws[:], T.xq[:, r * NC:(r + 1) * NC], plane(r),
                            True, True).then_inc(sem["mm%d" % r], 1)
+    if not home:
+        for j, t in enumerate(cross):
+            tile_here(t)
+            if t != k:
+                g.tensor.wait_ge(sem.wc, n_off)
+                g.tensor.wait_ge(sem.wp, n_off)
+            wq, ws = (T.wq, T.ws) if t == k else (T.wq2, T.ws2)
+            mm = g.tensor.matmul_mx(T.ps[:, k * BANK:k * BANK + NC], wq[:], ws[:], T.xq[:, t * NC:(t + 1) * NC], plane(t),
+                                    j == 0, j == len(cross) - 1)
+        mm.then_inc(sem["mm%d" % k], 1)
 
-    for r in order:
+    for r in shares:
         if r != k:
             g.scalar.wait_ge(sem["mm%d" % r], 1)
             g.scalar.activation(T.pout[:, r * NC:(r + 1) * NC], T.ps[:, r * BANK:r * BANK + NC],
@@ -106,24 +146,38 @@ def rank_program(g, core, T, topo):
                      pid, rid, m_off)
         sent[0] += n_off
 
+    def pass_on():
+        for t in straight:
+            g.wait_ge(sem["c%d" % t], n_off)
+            spread(codes, "c%d", t, [(buddies, m_on, t)])
+            g.wait_ge(sem["s%d" % t], n_off)
+            spread(plane, "s%d", t, [(buddies, m_on, t)])
+
     g.wait_ge(sem.qx, 1)
-    spread(codes, "c%d", i, gates, near)
-    spread(plane, "s%d", i, gates, near)
-    send_partial(i)
-    for r in straight:
-        g.wait_ge(sem["c%d" % r], n_off)
-        spread(codes, "c%d", r, [], near)
-        g.wait_ge(sem["s%d" % r], n_off)
-        spread(plane, "s%d", r, [], near)
-    for r in near + straight + passed:
-        send_partial(r)
+    spread(codes, "c%d", i, [(gates, m_off, there_slot), (buddies, m_on, i)])
+    spread(plane, "s%d", i, [(gates, m_off, there_slot), (buddies, m_on, i)])
+    if home:
+        send_partial(i)
+        pass_on()
+        for r in near + straight + passed:
+            send_partial(r)
+    else:
+        g.wait_ge(sem.qw, 1)
+        for c in swap:
+            rid, pid, _ = topo.addr(row[c])
+            g.remote_dma(T.wq2[:].bitcast(dt.uint8), T.wq[:].bitcast(dt.uint8), sem.wc, sem.sent, pid, rid, m_off)
+            g.remote_dma(T.ws2[:], T.ws[:], sem.wp, sem.sent, pid, rid, m_off)
+            sent[0] += 2 * n_off
+        for r in [i] + near:
+            send_partial(r)
+        pass_on()
     g.wait_ge(sem.sent, sent[0])
 
     def hops(c):
         a, b = topo.chip(row[c]), here
         return 1 if (topo.mates(a, b) or topo.same_plane(a, b)) else 2
 
-    srcs = sorted([c for c in range(GC) if c != k], key=lambda c: (hops(c), c))
+    srcs = sorted([c for c in range(GC) if c != k and c not in swap], key=lambda c: (hops(c), c))
     g.vector.wait_ge(sem["mm%d" % k], 1)
     for j, c in enumerate(srcs):
         g.vector.wait_ge(sem["p%d" % c], n_off)

from concourse.bass import DstId, RemoteDMATransfer
from concourse.mybir import dt, AluOpType, ActivationFunctionType

GR, GC, NC, BANK = 4, 4, 256, 512

SCRATCH = {
    "xb": ("sbuf", [128, 4 * NC], "bfloat16"),
    "wb": ("sbuf", [128, 512], "bfloat16"),
    "xq": ("sbuf", [128, GR * NC], "float8_e4m3fn_x4"),
    "xs": ("sbuf", [128, GR * NC], "uint8"),
    "wq": ("sbuf", [128, 128], "float8_e4m3fn_x4"),
    "ws": ("sbuf", [128, 128], "uint8"),
    "wq2": ("sbuf", [128, 128], "float8_e4m3fn_x4"),
    "ws2": ("sbuf", [128, 128], "uint8"),
    "ps": ("psum", [128, GR * BANK], "float32"),
    "pout": ("sbuf", [128, GR * NC], "float32"),
    "pin": ("sbuf", [128, GC * NC], "float32"),
    "acc": ("sbuf", [128, NC], "float32"),
}
SEMAPHORES = (["lx", "lw", "qx", "qw", "sent", "stored", "a0", "a1", "a2", "wc", "wp"]
              + ["c%d" % r for r in range(GR)] + ["s%d" % r for r in range(GR)]
              + ["mm%d" % r for r in range(GR)] + ["cp%d" % r for r in range(GR)]
              + ["p%d" % c for c in range(GC)])


def _bits(m):
    return bin(m).count("1")


def rank_program(g, core, T, topo):
    rank = T.rank_of(core)
    if rank is None:
        return
    i, k = divmod(rank, GC)
    sem = T.sem

    def rk(r, c):
        return T.cores[r * GC + c]

    def at_home(r, c):
        return topo.chip(rk(c, c)) == topo.chip(rk(r, c))

    def gate_of(src, takers):
        same_die = [c for c in takers if topo.die(c) == topo.die(src)]
        return (same_die or takers)[0]

    col = [rk(r, k) for r in range(GR)]
    row = [rk(i, c) for c in range(GC)]
    here = topo.chip(core)
    mine = [c for c in col if topo.chip(c) == here]
    near = [r for r in range(GR) if r != i and topo.chip(col[r]) == here]
    far = [r for r in range(GR) if topo.chip(col[r]) != here]
    home = at_home(i, k)
    buddies = [col[r] for r in near]

    if home:
        cross = list(far)
        src_of = dict((t, rk(t, k)) for t in cross)
    else:
        cross = [k] + [s for s in range(GC) if s != k and at_home(k, s)]
        src_of = dict((t, rk(k, t)) for t in cross)
    assert sorted(cross) == sorted(far) and len(cross) == 2
    straight = [t for t in cross if gate_of(src_of[t], mine) == core]
    passed = [t for t in cross if gate_of(src_of[t], mine) != core]

    if home:
        takers = [rk(f, i) for f in range(GR) if topo.chip(rk(f, i)) != topo.chip(rk(i, i))]
        there_slot = k
    else:
        takers = [col[f] for f in far]
        there_slot = i
    gates = [gate_of(core, [c for c in takers if topo.chip(c) == ch]) for ch in sorted(set(topo.chip(c) for c in takers))]
    swap = [] if home else [c for c in range(GC) if c != k and not at_home(i, c)]

    m_off = topo.mask(core, buddies[0])
    for c in T.cores:
        if topo.chip(c) != here:
            m_off &= topo.mask(core, c)
    m_on = topo.mask(core, buddies[0]) & ~m_off
    n_off, n_on = _bits(m_off), _bits(m_on)
    sent = [0]

    def dst_id(c):
        rid, pid, _ = topo.addr(c)
        return DstId(rid=rid, pnc=pid)

    def codes(r):
        return T.xq[:, r * NC:(r + 1) * NC].bitcast(dt.uint8)

    def plane(r):
        return T.xs[:, r * NC:(r + 1) * NC]

    def spread(view, name, slot, groups):
        tr = []
        for cores_, m, there in groups:
            if cores_:
                tr.append(RemoteDMATransfer(dst_ids=[dst_id(c) for c in cores_], dma_engine_mask=m,
                                            remote_sem=sem[name % there], srcs=[view(slot)],
                                            dsts=[view(there) for c in cores_]))
                sent[0] += _bits(m)
        g.remote_dma_fused(tr, local_sem=sem.sent)

    g.sync.dma_start(T.xb[:], T.x[:]).then_inc(sem.lx, 16)
    g.scalar.dma_start(T.wb[:], T.w[:]).then_inc(sem.lw, 16)
    g.vector.wait_ge(sem.lx, 16)
    g.vector.quantize_mx(T.xq[:, i * NC:(i + 1) * NC], plane(i), T.xb[:]).then_inc(sem.qx, 1)
    g.vector.wait_ge(sem.lw, 16)
    g.vector.quantize_mx(T.wq[:], T.ws[:], T.wb[:]).then_inc(sem.qw, 1)

    def tile_here(t):
        n = n_off if t in straight else n_on
        g.tensor.wait_ge(sem["c%d" % t], n)
        g.tensor.wait_ge(sem["s%d" % t], n)

    g.tensor.wait_ge(sem.qx, 1)
    g.tensor.wait_ge(sem.qw, 1)
    shares = [i] + near + (straight + passed if home else [])
    for r in shares:
        if r != i:
            tile_here(r)
        g.tensor.matmul_mx(T.ps[:, r * BANK:r * BANK + NC], T.wq[:], T.ws[:], T.xq[:, r * NC:(r + 1) * NC], plane(r),
                           True, True).then_inc(sem["mm%d" % r], 1)
    if not home:
        for j, t in enumerate(cross):
            tile_here(t)
            if t != k:
                g.tensor.wait_ge(sem.wc, n_off)
                g.tensor.wait_ge(sem.wp, n_off)
            wq, ws = (T.wq, T.ws) if t == k else (T.wq2, T.ws2)
            mm = g.tensor.matmul_mx(T.ps[:, k * BANK:k * BANK + NC], wq[:], ws[:], T.xq[:, t * NC:(t + 1) * NC], plane(t),
                                    j == 0, j == len(cross) - 1)
        mm.then_inc(sem["mm%d" % k], 1)

    for r in shares:
        if r != k:
            g.scalar.wait_ge(sem["mm%d" % r], 1)
            g.scalar.activation(T.pout[:, r * NC:(r + 1) * NC], T.ps[:, r * BANK:r * BANK + NC],
                                ActivationFunctionType.Copy).then_inc(sem["cp%d" % r], 1)

    def send_partial(r):
        if r == k:
            return
        rid, pid, _ = topo.addr(row[r])
        g.wait_ge(sem["cp%d" % r], 1)
        g.remote_dma(T.pin[:, k * NC:(k + 1) * NC], T.pout[:, r * NC:(r + 1) * NC], sem["p%d" % k], sem.sent,
                     pid, rid, m_off)
        sent[0] += n_off

    def pass_on():
        for t in straight:
            g.wait_ge(sem["c%d" % t], n_off)
            spread(codes, "c%d", t, [(buddies, m_on, t)])
            g.wait_ge(sem["s%d" % t], n_off)
            spread(plane, "s%d", t, [(buddies, m_on, t)])

    g.wait_ge(sem.qx, 1)
    spread(codes, "c%d", i, [(gates, m_off, there_slot), (buddies, m_on, i)])
    spread(plane, "s%d", i, [(gates, m_off, there_slot), (buddies, m_on, i)])
    if home:
        send_partial(i)
        pass_on()
        for r in near + straight + passed:
            send_partial(r)
    else:
        g.wait_ge(sem.qw, 1)
        for c in swap:
            rid, pid, _ = topo.addr(row[c])
            g.remote_dma(T.wq2[:].bitcast(dt.uint8), T.wq[:].bitcast(dt.uint8), sem.wc, sem.sent, pid, rid, m_off)
            g.remote_dma(T.ws2[:], T.ws[:], sem.wp, sem.sent, pid, rid, m_off)
            sent[0] += 2 * n_off
        for r in [i] + near:
            send_partial(r)
        pass_on()
    g.wait_ge(sem.sent, sent[0])

    def hops(c):
        a, b = topo.chip(row[c]), here
        return 1 if (topo.mates(a, b) or topo.same_plane(a, b)) else 2

    srcs = sorted([c for c in range(GC) if c != k and c not in swap], key=lambda c: (hops(c), c))
    g.vector.wait_ge(sem["mm%d" % k], 1)
    for j, c in enumerate(srcs):
        g.vector.wait_ge(sem["p%d" % c], n_off)
        if j:
            g.vector.wait_ge(sem["a%d" % (j - 1)], 1)
        first = T.ps[:, k * BANK:k * BANK + NC] if j == 0 else T.acc[:]
        g.vector.tensor_tensor(T.acc[:], first, T.pin[:, c * NC:(c + 1) * NC], AluOpType.add).then_inc(sem["a%d" % j], 1)

    g.sync.wait_ge(sem["a%d" % (len(srcs) - 1)], 1)
    g.sync.dma_start(T.y[:], T.acc[:]).then_inc(sem.stored, 16)
    g.sync.wait_ge(sem.stored, 16)
